import numpy as np
import ml_dtypes


def mxq(x, axis, fmt="e4m3"):
    dtype, down = {"e4m3": (ml_dtypes.float8_e4m3fn, 7), "e5m2": (ml_dtypes.float8_e5m2, 14)}[fmt]
    v = np.moveaxis(np.asarray(x, np.float32).astype(ml_dtypes.bfloat16).astype(np.float64), axis, -1)
    blocks = v.reshape(v.shape[:-1] + (-1, 32))
    amax = np.abs(blocks).max(-1, keepdims=True)
    byte = np.maximum(np.where(amax > 0, np.frexp(amax)[1] - 1 + 127, 0) - down, 1)
    scale = np.exp2(byte - 127.0)
    codes = (blocks / scale).astype(np.float32).astype(dtype).astype(np.float64)
    return np.moveaxis((codes * scale).reshape(v.shape), -1, axis)


WIDE = False


def mx_kscale(k):
    if not WIDE:
        return np.ones(k)
    levels = np.array([10, -10, 5, -5, 0])
    if k % 512:
        return np.exp2(np.random.permutation(np.resize(levels, k // 32))).repeat(32)
    a = np.empty((k // 512, 16))
    for p in range(k // 512):
        a[p, :8] = np.random.permutation(np.resize(levels, 8))
        for g in range(8):
            far = levels[np.abs(levels - a[p, g]) >= 10]
            a[p, g + 8] = far[np.random.randint(len(far))]
    return np.exp2(a.ravel()).repeat(32)


def f64(x):
    return np.asarray(x).astype(np.float64)


def striped(idx):
    return np.tile(np.asarray(idx).reshape(-1, 16).T, (8, 1)).astype(np.uint16)


def unstriped(offs):
    return offs[:16].T.reshape(-1).astype(np.int64)


E2M1 = np.array([0.0, 0.5, 1.0, 1.5, 2.0, 3.0, 4.0, 6.0, -0.0, -0.5, -1.0, -1.5, -2.0, -3.0, -4.0, -6.0])


def pack_weight(w, fmt):
    k, n = w.shape
    w = f64(np.asarray(w, np.float32).astype(ml_dtypes.bfloat16)).reshape(k // 32, 32, n)
    amax = np.abs(w).max(1)
    if fmt == "e4m3":
        byte = np.frexp(amax)[1] - 1 + 127 - 7
    else:
        mant, ex = np.frexp(amax / 6.0)
        byte = np.where(mant > 0.5, ex, ex - 1) + 127
    byte = np.clip(np.where(amax > 0, byte, 1), 1, 254)
    scaled = (w * np.exp2(127.0 - byte)[:, None, :]).reshape(k, n).astype(np.float32)
    by_word = np.ascontiguousarray(scaled.reshape(k // 512, 128, 4, n).transpose(0, 1, 3, 2))
    if fmt == "e4m3":
        words = by_word.astype(ml_dtypes.float8_e4m3fn).view(np.uint8)
    else:
        c = by_word.astype(ml_dtypes.float4_e2m1fn).view(np.uint8) & 0xF
        words = (c[..., 0::2] | (c[..., 1::2] << 4)).reshape(k // 512, 128, 2 * n)
    return np.ascontiguousarray(words), np.ascontiguousarray(byte.astype(np.uint8).reshape(k // 512, 16, n))


def unpack_weight(words, scales, fmt):
    g, _, n = scales.shape
    words = np.ascontiguousarray(words).reshape(g, 128, n, -1)
    if fmt == "e4m3":
        vals = words.view(ml_dtypes.float8_e4m3fn).astype(np.float64)
    else:
        nib = np.empty((g, 128, n, 4), np.uint8)
        nib[..., 0::2] = words & 0xF
        nib[..., 1::2] = words >> 4
        vals = E2M1[nib]
    vals = vals * np.repeat(np.exp2(scales.astype(np.float64) - 127.0), 8, axis=1)[..., None]
    return vals.transpose(0, 1, 3, 2).reshape(g * 512, n)


def sigmoid(v):
    return 1.0 / (1.0 + np.exp(-v))


def bf(x):
    return np.asarray(x, np.float32).astype(ml_dtypes.bfloat16)


def planes(Y):
    r, m = Y.shape
    b = f64(bf(Y)).reshape(r // 32, 32, m)
    amax = np.abs(b).max(1)
    byte = np.clip(np.where(amax > 0, np.frexp(amax)[1] - 1 + 127 - 7, 1), 1, 254)
    codes = (b * np.exp2(127.0 - byte)[:, None, :]).reshape(r, m).astype(np.float32).astype(ml_dtypes.float8_e4m3fn).view(np.uint8)
    words = codes.reshape(r // 512, 128, 4, m).transpose(0, 1, 3, 2)
    return np.ascontiguousarray(words), np.ascontiguousarray(byte.astype(np.uint8).reshape(r // 512, 16, m))


D, T, I, Q, E, M = 512, 2048, 512, 256, 512, 512


def setup_inputs():
    n = np.random.standard_normal
    idx = np.random.permutation(T)[:I]
    fd = mx_kscale(D)
    fm = mx_kscale(M)
    fi = mx_kscale(I)
    ti = np.ones(T)
    ti[idx] = fi
    keysp = pack_weight(n((D, T)) / fd[:, None], "e2m1")
    return {
        "query": (n((D, Q)) * 0.4 / np.sqrt(D) * fd[:, None]).astype(np.float32),
        "wkey": (n((D, M)) / fd[:, None]).astype(np.float32),
        "wval": (n((M, E)) / fm[:, None]).astype(np.float32),
        "keys_words": keysp[0],
        "keys_scales": keysp[1],
        "vals": (n((E, T)) / ti).astype(np.float32),
        "th": (np.random.uniform(0.8, 1.6, (Q, 1))).astype(np.float32),
        "steep": (np.random.uniform(1.0, 3.0, (Q, 1))).astype(np.float32),
        "wf": (np.random.uniform(0.5, 2.0, (1, M)) * fm).astype(np.float32),
        "size": (np.random.uniform(0.5, 2.0, (1, I)) * fi).astype(np.float32),
        "offs": striped(idx),
    }


def reference(query, wkey, wval, keys_words, keys_scales, vals, th, steep, wf, size, offs):
    idx = unstriped(offs)
    keysu = unpack_weight(keys_words, keys_scales, "e2m1")
    queryq = mxq(f64(query), 0, "e4m3")
    wkeyq = mxq(f64(wkey), 0, "e4m3")
    a = queryq.T @ wkeyq
    keysidxg = keysu[:, idx]
    b = queryq.T @ keysidxg
    z = np.max(b, axis=1, keepdims=True)
    g = sigmoid(f64(steep) * (z - f64(th)))
    p = np.exp(a - np.max(a, axis=1, keepdims=True))
    w = p * f64(wf) * (1.0 - g) / np.sum(p, axis=1, keepdims=True)
    wt = w.T
    r = np.exp(b - z)
    u = r * f64(size) * g / np.sum(r, axis=1, keepdims=True)
    ut = u.T
    vt = f64(vals)[:, idx].T
    wvalq = mxq(f64(wval), 0, "e4m3")
    wtq = mxq(wt, 0, "e4m3")
    vtq = mxq(vt, 0, "e4m3")
    utq = mxq(ut, 0, "e4m3")
    o = wvalq.T @ wtq + vtq.T @ utq
    words, scales = planes(o)
    return o, words, scales

@@ -1,0 +1,265 @@
+from contextlib import ExitStack
+
+import concourse.mybir as mybir
+from concourse.masks import make_identity
+
+D, T, I, Q, E, M = 512, 2048, 512, 256, 512, 512
+FLOPS = 2 * 512 * 512 * 256 * 4
+
+F32 = mybir.dt.float32
+BF16 = mybir.dt.bfloat16
+I32 = mybir.dt.int32
+U32 = mybir.dt.uint32
+U16 = mybir.dt.uint16
+U8 = mybir.dt.uint8
+FP8X4 = mybir.dt.float8_e4m3fn_x4
+FP4X4 = mybir.dt.float4_e2m1fn_x4
+ALU = mybir.AluOpType
+ACT = mybir.ActivationFunctionType
+AX = mybir.AxisListType
+
+P = 128
+PACK = 4
+QT = Q // P
+
+
+def tile_attend_confidencegate_pl_kernel(
+    tc, query, wkey, wval, keys_words, keys_scales, vals, th, steep, wf, size, offs, out_0, out_1, out_2
+):
+    nc = tc.nc
+    with ExitStack() as ctx:
+        sb = ctx.enter_context(tc.tile_pool(name="sb", bufs=1))
+        ps = ctx.enter_context(tc.psum_pool(name="ps", bufs=1))
+
+        def tile(shape, dtype, name, tag=None):
+            return sb.tile(shape, dtype, name=name, tag=tag or name, align_bytes=64)
+
+        def bank(tag, name):
+            return ps.tile([P, 512], F32, name=name, tag=tag)
+
+        def quantise(src, name, cols):
+            codes = tile([P, cols], U32, name + "_codes")
+            scales = tile([P, cols], U8, name + "_scales")
+            nc.vector.quantize_mx(out=codes[:].bitcast(FP8X4), scales=scales[:], in_=src)
+            return codes, scales
+
+        key_scale_pool = tile([P, T], U8, "key_scale_pool")
+        nc.gpsimd.memset(key_scale_pool[:, 0 : T // 2].bitcast(I32), 0)
+        nc.vector.memset(key_scale_pool[:, T // 2 : T].bitcast(I32), 0)
+        ident = tile([P, P], F32, "ident")
+        make_identity(nc, ident[:])
+
+        offsets = tile([P, I // 16], U16, "offsets")
+        nc.sync.dma_start(offsets[:], offs)
+        key_pool = tile([P, T], U16, "key_pool")
+        nc.sync.dma_start(key_pool[:].bitcast(I32), keys_words[0].bitcast(I32))
+        query_raw = tile([P, PACK, Q], F32, "query_raw")
+        nc.sync.dma_start(query_raw[:], query.rearrange("(p j) q -> p j q", j=PACK))
+        for quad in range(4):
+            nc.sync.dma_start(
+                key_scale_pool[32 * quad : 32 * quad + 4, :].bitcast(I32),
+                keys_scales[0, 4 * quad : 4 * quad + 4, :].bitcast(I32),
+            )
+        wkey_rows = wkey.rearrange("(p j) m -> p j m", j=PACK)
+        wkey_raw = [tile([P, PACK, M // 2], F32, "wkey_raw%d" % half) for half in range(2)]
+        for half in range(2):
+            nc.sync.dma_start(wkey_raw[half][:], wkey_rows[:, :, half * M // 2 : (half + 1) * M // 2])
+        steep_t = tile([P, QT], F32, "steep_t")
+        th_t = tile([P, QT], F32, "th_t")
+        size_c = tile([P, PACK], F32, "size_c")
+        wf_c = tile([P, PACK], F32, "wf_c")
+        nc.sync.dma_start(steep_t[:], steep.rearrange("(x j) o -> x (j o)", j=QT))
+        nc.sync.dma_start(th_t[:], th.rearrange("(x j) o -> x (j o)", j=QT))
+        nc.sync.dma_start(size_c[:], size.rearrange("o (x k) -> (o x) k", k=PACK))
+        nc.sync.dma_start(wf_c[:], wf.rearrange("o (x k) -> (o x) k", k=PACK))
+        wval_raw = tile([P, PACK, E], F32, "wval_raw")
+        nc.sync.dma_start(wval_raw[:], wval.rearrange("(p j) e -> p j e", j=PACK))
+        vals_dealt = vals.rearrange("(s r) t -> r s t", r=PACK)
+        reused = ["val_pool%d" % r for r in range(PACK)]
+        val_pool = [tile([P, T], F32, reused[r]) for r in range(PACK)]
+        for r in range(PACK):
+            nc.sync.dma_start(val_pool[r][:], vals_dealt[r])
+        th_c, steep_c = th_t[:], steep_t[:]
+
+        size_all = bank("size", "size_all")
+        wf_all = bank("wf", "wf_all")
+        for k in range(4):
+            nc.tensor.transpose(size_all[:, P * k : P * (k + 1)], size_c[:, k : k + 1].to_broadcast([P, P]), ident[:])
+        for k in range(4):
+            nc.tensor.transpose(wf_all[:, P * k : P * (k + 1)], wf_c[:, k : k + 1].to_broadcast([P, P]), ident[:])
+        neg_steep = tile([P, QT], F32, "neg_steep")
+        steep_th = tile([P, QT], F32, "steep_th")
+        neg_steep_th = tile([P, QT], F32, "neg_steep_th")
+        nc.gpsimd.tensor_scalar(neg_steep[:], steep_c, -1.0, 0.0, ALU.mult, ALU.add)
+        nc.gpsimd.tensor_tensor(steep_th[:], steep_c, th_c, ALU.mult)
+        nc.gpsimd.tensor_tensor(neg_steep_th[:], neg_steep[:], th_c, ALU.mult)
+
+        key_words = tile([P, I], U16, "key_words")
+        nc.vector.tensor_copy(key_words[:], key_pool[:].indirect(offsets[:]))
+        key_scales = tile([P, I], U8, "key_scales")
+        nc.vector.tensor_copy(key_scales[:], key_scale_pool[:].indirect(offsets[:]))
+        query_bf = tile([P, Q, PACK], BF16, "query_bf")
+        nc.scalar.activation(
+            query_bf[:].rearrange("p (j x) t -> p x t j", j=QT),
+            query_raw[:].rearrange("p t (x j) -> p x t j", j=QT),
+            ACT.Copy,
+        )
+        q_codes, q_scales = quantise(query_bf[:].rearrange("p c t -> p (c t)"), "query", Q)
+
+        score_b = [bank("sb%d" % j, "score_b%d" % j) for j in range(QT)]
+        for j in range(QT):
+            qs = slice(P * j, P * (j + 1))
+            nc.tensor.matmul_mx(
+                score_b[j][:], q_codes[:, qs].bitcast(FP8X4), q_scales[:, qs],
+                key_words[:].bitcast(FP4X4), key_scales[:], start=True, stop=True,
+            )
+
+        wk_codes = tile([P, M], U32, "wk_codes")
+        wk_scales = tile([P, M], U8, "wk_scales")
+        for half, copy in enumerate((nc.vector.tensor_copy, nc.scalar.copy)):
+            ms = slice(half * M // 2, (half + 1) * M // 2)
+            wk_bf = tile([P, M // 2, PACK], BF16, "wk_bf%d" % half)
+            copy(
+                wk_bf[:].rearrange("p (c i) t -> p c t i", i=4),
+                wkey_raw[half][:].rearrange("p t (c i) -> p c t i", i=4),
+            )
+            nc.vector.quantize_mx(
+                out=wk_codes[:, ms].bitcast(FP8X4), scales=wk_scales[:, ms], in_=wk_bf[:].rearrange("p c t -> p (c t)")
+            )
+        score_a = [bank("sa%d" % j, "score_a%d" % j) for j in range(QT)]
+        for j in range(QT):
+            qs = slice(P * j, P * (j + 1))
+            nc.tensor.matmul_mx(
+                score_a[j][:], q_codes[:, qs].bitcast(FP8X4), q_scales[:, qs],
+                wk_codes[:].bitcast(FP8X4), wk_scales[:], start=True, stop=True,
+            )
+
+        def exps(score, name):
+            neg_max = tile([P, QT], F32, name + "_neg_max")
+            sums = tile([P, QT], F32, name + "_sums")
+            probs = [tile([P, 512], F32, name + "_probs%d" % j) for j in range(QT)]
+            for j in range(QT):
+                nc.vector.tensor_reduce(neg_max[:, j : j + 1], score[j][:], AX.X, ALU.max, negate=True)
+                nc.scalar.activation(
+                    probs[j][:], score[j][:], ACT.Exp, bias=neg_max[:, j : j + 1], accum_out=sums[:, j : j + 1]
+                )
+            return neg_max, sums, probs
+
+        def weights(probs, sums, odds, factor_all, tag, slot, name):
+            den = tile([P, QT], F32, name + "_den")
+            coef = tile([P, QT], F32, name + "_coef")
+            nc.vector.scalar_tensor_tensor(den[:], odds[:], 1.0, sums[:], ALU.add, ALU.mult)
+            nc.vector.reciprocal(coef[:], den[:])
+            turned_w = bank(tag, name + "_turned")
+            view = turned_w[:].rearrange("p (u q) -> p u q", u=2)
+            for j in range(QT):
+                w_bf = tile([P, 512], BF16, name + "_bf%d" % j)
+                nc.vector.scalar_tensor_tensor(
+                    w_bf[:].rearrange("p (x k) -> p x k", k=PACK),
+                    probs[j][:].rearrange("p (x k) -> p x k", k=PACK),
+                    coef[:, j : j + 1],
+                    factor_all[:].rearrange("p (k x) -> p x k", k=PACK),
+                    ALU.mult,
+                    ALU.mult,
+                )
+                words = w_bf[:].bitcast(F32)
+                for u in range(2):
+                    nc.tensor.transpose(view[:, u, P * j : P * (j + 1)], words[:, u::2], ident[:])
+            woven = tile([P, Q, 2], F32, name + "_woven", tag=slot)
+            nc.scalar.copy(
+                woven[:].rearrange("p (x j) u -> p x j u", j=QT), view.rearrange("p u (j x) -> p x j u", j=QT)
+            )
+            return quantise(woven[:].rearrange("p q u -> p (q u)").bitcast(BF16), name, Q)
+
+        neg_z, sum_b, probs_b = exps(score_b, "b")
+        odds_against = tile([P, QT], F32, "odds_against")
+        odds_for = tile([P, QT], F32, "odds_for")
+        for j in range(QT):
+            c = slice(j, j + 1)
+            nc.scalar.activation(odds_against[:, c], neg_z[:, c], ACT.Exp, bias=steep_th[:, c], scale=steep_c[:, c])
+            nc.scalar.activation(odds_for[:, c], neg_z[:, c], ACT.Exp, bias=neg_steep_th[:, c], scale=neg_steep[:, c])
+        neg_max_a, sum_a, probs_a = exps(score_a, "a")
+
+        wv_bf = tile([P, PACK, P, PACK], BF16, "wv_bf", tag="wk_codes")
+        for piece in range(4):
+            ss = slice(32 * piece, 32 * (piece + 1))
+            nc.gpsimd.tensor_copy(
+                wv_bf[:].rearrange("p r s j -> p s j r")[:, ss],
+                wval_raw[:].rearrange("p j (s r) -> p s j r", r=PACK)[:, ss],
+            )
+
+        def values(r, tag, shared, slot):
+            picked = tile([P, I], BF16, "picked%d" % r, tag=slot)
+            if shared:
+                nc.scalar.activation(picked[:, 0:256], val_pool[r][:].indirect(offsets[:, 0:16]), ACT.Copy)
+                nc.vector.tensor_copy(picked[:, 256:512], val_pool[r][:].indirect(offsets[:, 16:32]))
+            else:
+                nc.scalar.activation(picked[:], val_pool[r][:].indirect(offsets[:]), ACT.Copy)
+            turned_v = bank(tag, "turned_v%d" % r)
+            view = turned_v[:, 0:256].rearrange("p (u s) -> p u s", u=2)
+            words = picked[:].bitcast(F32)
+            for u in range(2):
+                nc.tensor.transpose(view[:, u, :], words[:, u::2], ident[:])
+            woven = tile([P, P, 2], F32, "v_woven%d" % r)
+            nc.scalar.copy(woven[:], view.rearrange("p u s -> p s u"))
+            return quantise(woven[:].rearrange("p s u -> p (s u)").bitcast(BF16), "v%d" % r, P)
+
+        v_mx = [values(0, "vt", False, "a_neg_max")]
+        u_codes, u_scales = weights(probs_b, sum_b, odds_against, size_all, "sb0", reused[0], "u")
+        v_mx.append(values(1, "sb1", False, "u_bf1"))
+        w_codes, w_scales = weights(probs_a, sum_a, odds_for, wf_all, "vt", reused[1], "w")
+        wv_codes, wv_scales = quantise(wv_bf[:].rearrange("p r s j -> p (r s j)"), "wval", E)
+        v_mx.append(values(2, "size", True, "w_bf1"))
+
+        result = [bank("sa%d" % h, "result%d" % h) for h in range(QT)]
+
+        def products(r):
+            es = slice(P * r, P * (r + 1))
+            v_codes, v_scales = v_mx[r]
+            for h in range(QT):
+                qs = slice(P * h, P * (h + 1))
+                nc.tensor.matmul_mx(
+                    result[h][:, es], wv_codes[:, es].bitcast(FP8X4), wv_scales[:, es],
+                    w_codes[:, qs].bitcast(FP8X4), w_scales[:, qs], start=True, stop=False,
+                )
+                nc.tensor.matmul_mx(
+                    result[h][:, es], v_codes[:].bitcast(FP8X4), v_scales[:],
+                    u_codes[:, qs].bitcast(FP8X4), u_scales[:, qs], start=False, stop=True,
+                )
+
+        last = PACK - 1
+        for r in range(2):
+            products(r)
+        v_mx.append(values(last, "wf", True, reused[1]))
+        out_dealt = out_0.rearrange("(s r) q -> s r q", r=PACK)
+        o_first = tile([P, 2, Q], F32, "o_first")
+        for h in range(QT):
+            nc.vector.tensor_copy(
+                o_first[:, :, P * h : P * (h + 1)], result[h][:, 0 : P * 2].rearrange("p (r q) -> p r q", r=2)
+            )
+        nc.sync.dma_start(out_dealt[:, 0:2, :], o_first[:])
+        for r in range(2, PACK):
+            products(r)
+
+        o_codes = tile([P, Q], U32, "o_codes")
+        o_scales = tile([P, Q], U8, "o_scales")
+        for h, copy in enumerate((nc.vector.tensor_copy, nc.scalar.copy)):
+            qs = slice(P * h, P * (h + 1))
+            o_bf = tile([P, P, PACK], BF16, "o_bf%d" % h)
+            copy(o_bf[:], result[h][:].rearrange("p (r q) -> p q r", r=PACK))
+            nc.vector.quantize_mx(
+                out=o_codes[:, qs].bitcast(FP8X4), scales=o_scales[:, qs], in_=o_bf[:].rearrange("p q r -> p (q r)")
+            )
+        o_last = tile([P, 2, Q], F32, "o_last")
+        for h in range(QT):
+            nc.scalar.copy(
+                o_last[:, :, P * h : P * (h + 1)], result[h][:, P * 2 : P * PACK].rearrange("p (r q) -> p r q", r=2)
+            )
+        nc.sync.dma_start(out_dealt[:, 2:PACK, :], o_last[:])
+
+        nc.sync.dma_start(out_1[0].rearrange("p c t -> p (c t)").bitcast(I32), o_codes[:].bitcast(I32))
+        for quad in range(4):
+            queue = nc.scalar if quad % 2 else nc.sync
+            queue.dma_start(
+                out_2[0, 4 * quad : 4 * quad + 4, :].bitcast(I32), o_scales[32 * quad : 32 * quad + 4, :].bitcast(I32)
+            )

@@ -37,8 +37,8 @@ def tile_attend_confidencegate_pl_kernel(
         def bank(tag, name):
             return ps.tile([P, 512], F32, name=name, tag=tag)
 
-        def quantise(src, name, cols):
-            codes = tile([P, cols], U32, name + "_codes")
+        def quantise(src, name, cols, slot=None):
+            codes = tile([P, cols], U32, name + "_codes", tag=slot)
             scales = tile([P, cols], U8, name + "_scales")
             nc.vector.quantize_mx(out=codes[:].bitcast(FP8X4), scales=scales[:], in_=src)
             return codes, scales
@@ -116,10 +116,10 @@ def tile_attend_confidencegate_pl_kernel(
 
         wk_codes = tile([P, M], U32, "wk_codes")
         wk_scales = tile([P, M], U8, "wk_scales")
-        for half, copy in enumerate((nc.vector.tensor_copy, nc.scalar.copy)):
+        for half in range(2):
             ms = slice(half * M // 2, (half + 1) * M // 2)
             wk_bf = tile([P, M // 2, PACK], BF16, "wk_bf%d" % half)
-            copy(
+            nc.scalar.copy(
                 wk_bf[:].rearrange("p (c i) t -> p c t i", i=4),
                 wkey_raw[half][:].rearrange("p t (c i) -> p c t i", i=4),
             )
@@ -148,7 +148,9 @@ def tile_attend_confidencegate_pl_kernel(
         def weights(probs, sums, odds, factor_all, tag, slot, name):
             den = tile([P, QT], F32, name + "_den")
             coef = tile([P, QT], F32, name + "_coef")
-            nc.vector.scalar_tensor_tensor(den[:], odds[:], 1.0, sums[:], ALU.add, ALU.mult)
+            odds_1 = tile([P, QT], F32, name + "_odds_1")
+            nc.gpsimd.tensor_scalar(odds_1[:], odds[:], 1.0, 1.0, ALU.mult, ALU.add)
+            nc.gpsimd.tensor_tensor(den[:], odds_1[:], sums[:], ALU.mult)
             nc.vector.reciprocal(coef[:], den[:])
             turned_w = bank(tag, name + "_turned")
             view = turned_w[:].rearrange("p (u q) -> p u q", u=2)
@@ -180,14 +182,6 @@ def tile_attend_confidencegate_pl_kernel(
             nc.scalar.activation(odds_for[:, c], neg_z[:, c], ACT.Exp, bias=neg_steep_th[:, c], scale=neg_steep[:, c])
         neg_max_a, sum_a, probs_a = exps(score_a, "a")
 
-        wv_bf = tile([P, PACK, P, PACK], BF16, "wv_bf", tag="wk_codes")
-        for piece in range(4):
-            ss = slice(32 * piece, 32 * (piece + 1))
-            nc.gpsimd.tensor_copy(
-                wv_bf[:].rearrange("p r s j -> p s j r")[:, ss],
-                wval_raw[:].rearrange("p j (s r) -> p s j r", r=PACK)[:, ss],
-            )
-
         def values(r, tag, shared, slot):
             picked = tile([P, I], BF16, "picked%d" % r, tag=slot)
             if shared:
@@ -202,14 +196,18 @@ def tile_attend_confidencegate_pl_kernel(
                 nc.tensor.transpose(view[:, u, :], words[:, u::2], ident[:])
             woven = tile([P, P, 2], F32, "v_woven%d" % r)
             nc.scalar.copy(woven[:], view.rearrange("p u s -> p s u"))
-            return quantise(woven[:].rearrange("p s u -> p (s u)").bitcast(BF16), "v%d" % r, P)
+            return woven[:].rearrange("p s u -> p (s u)").bitcast(BF16)
 
-        v_mx = [values(0, "vt", False, "a_neg_max")]
+        v_mx = [quantise(values(0, "vt", False, "a_neg_max"), "v0", P)]
         u_codes, u_scales = weights(probs_b, sum_b, odds_against, size_all, "sb0", reused[0], "u")
-        v_mx.append(values(1, "sb1", False, "u_bf1"))
+        v_mx.append(quantise(values(1, "sb1", False, "u_bf1"), "v1", P))
         w_codes, w_scales = weights(probs_a, sum_a, odds_for, wf_all, "vt", reused[1], "w")
+        wv_bf = tile([P, PACK, P, PACK], BF16, "wv_bf", tag="a_probs1")
+        nc.vector.tensor_copy(
+            wv_bf[:].rearrange("p r s j -> p s j r"), wval_raw[:].rearrange("p j (s r) -> p s j r", r=PACK)
+        )
         wv_codes, wv_scales = quantise(wv_bf[:].rearrange("p r s j -> p (r s j)"), "wval", E)
-        v_mx.append(values(2, "size", True, "w_bf1"))
+        v2_bf = values(2, "size", True, "w_bf1")
 
         result = [bank("sa%d" % h, "result%d" % h) for h in range(QT)]
 
@@ -230,7 +228,9 @@ def tile_attend_confidencegate_pl_kernel(
         last = PACK - 1
         for r in range(2):
             products(r)
-        v_mx.append(values(last, "wf", True, reused[1]))
+        v3_bf = values(last, "wf", True, reused[1])
+        v_mx.append(quantise(v2_bf, "v2", P, slot=reused[1]))
+        v_mx.append(quantise(v3_bf, "v3", P))
         out_dealt = out_0.rearrange("(s r) q -> s r q", r=PACK)
         o_first = tile([P, 2, Q], F32, "o_first")
         for h in range(QT):

@@ -21,6 +21,7 @@ AX = mybir.AxisListType
 P = 128
 PACK = 4
 QT = Q // P
+POOL_BYTES = 4 * T
 
 
 def tile_attend_confidencegate_pl_kernel(
@@ -29,16 +30,23 @@ def tile_attend_confidencegate_pl_kernel(
     nc = tc.nc
     with ExitStack() as ctx:
         sb = ctx.enter_context(tc.tile_pool(name="sb", bufs=1))
+        shared = ctx.enter_context(tc.tile_pool(name="shared", bufs=1))
         ps = ctx.enter_context(tc.psum_pool(name="ps", bufs=1))
 
         def tile(shape, dtype, name, tag=None):
             return sb.tile(shape, dtype, name=name, tag=tag or name, align_bytes=64)
 
+        def placed(shape, dtype, name, offset):
+            return shared.tile(shape, dtype, name=name, tag=name, offset=offset, align_bytes=64)
+
         def bank(tag, name):
             return ps.tile([P, 512], F32, name=name, tag=tag)
 
-        def quantise(src, name, cols, slot=None):
-            codes = tile([P, cols], U32, name + "_codes", tag=slot)
+        def quantise(src, name, cols, offset=None):
+            if offset is None:
+                codes = tile([P, cols], U32, name + "_codes")
+            else:
+                codes = placed([P, cols], U32, name + "_codes", offset)
             scales = tile([P, cols], U8, name + "_scales")
             nc.vector.quantize_mx(out=codes[:].bitcast(FP8X4), scales=scales[:], in_=src)
             return codes, scales
@@ -75,18 +83,12 @@ def tile_attend_confidencegate_pl_kernel(
         wval_raw = tile([P, PACK, E], F32, "wval_raw")
         nc.sync.dma_start(wval_raw[:], wval.rearrange("(p j) e -> p j e", j=PACK))
         vals_dealt = vals.rearrange("(s r) t -> r s t", r=PACK)
-        reused = ["val_pool%d" % r for r in range(PACK)]
-        val_pool = [tile([P, T], F32, reused[r]) for r in range(PACK)]
+        val_pool = [tile([P, T], F32, "val_pool0")]
+        val_pool.extend(placed([P, T], F32, "val_pool%d" % r, POOL_BYTES * (r - 1)) for r in range(1, PACK))
         for r in range(PACK):
             nc.sync.dma_start(val_pool[r][:], vals_dealt[r])
         th_c, steep_c = th_t[:], steep_t[:]
 
-        size_all = bank("size", "size_all")
-        wf_all = bank("wf", "wf_all")
-        for k in range(4):
-            nc.tensor.transpose(size_all[:, P * k : P * (k + 1)], size_c[:, k : k + 1].to_broadcast([P, P]), ident[:])
-        for k in range(4):
-            nc.tensor.transpose(wf_all[:, P * k : P * (k + 1)], wf_c[:, k : k + 1].to_broadcast([P, P]), ident[:])
         neg_steep = tile([P, QT], F32, "neg_steep")
         steep_th = tile([P, QT], F32, "steep_th")
         neg_steep_th = tile([P, QT], F32, "neg_steep_th")
@@ -134,10 +136,10 @@ def tile_attend_confidencegate_pl_kernel(
                 wk_codes[:].bitcast(FP8X4), wk_scales[:], start=True, stop=True,
             )
 
-        def exps(score, name):
+        def exps(score, name, slot):
             neg_max = tile([P, QT], F32, name + "_neg_max")
             sums = tile([P, QT], F32, name + "_sums")
-            probs = [tile([P, 512], F32, name + "_probs%d" % j) for j in range(QT)]
+            probs = [tile([P, 512], F32, name + "_probs0", tag=slot), tile([P, 512], F32, name + "_probs1")]
             for j in range(QT):
                 nc.vector.tensor_reduce(neg_max[:, j : j + 1], score[j][:], AX.X, ALU.max, negate=True)
                 nc.scalar.activation(
@@ -145,12 +147,15 @@ def tile_attend_confidencegate_pl_kernel(
                 )
             return neg_max, sums, probs
 
-        def weights(probs, sums, odds, factor_all, tag, slot, name):
+        def denominators(odds, sums, name):
             den = tile([P, QT], F32, name + "_den")
-            coef = tile([P, QT], F32, name + "_coef")
-            odds_1 = tile([P, QT], F32, name + "_odds_1")
-            nc.gpsimd.tensor_scalar(odds_1[:], odds[:], 1.0, 1.0, ALU.mult, ALU.add)
-            nc.gpsimd.tensor_tensor(den[:], odds_1[:], sums[:], ALU.mult)
+            for j in range(QT):
+                c = slice(j, j + 1)
+                nc.scalar.activation(den[:, c], odds[:, c], ACT.Identity, bias=sums[:, c], scale=sums[:, c])
+            return den
+
+        def weights(probs, den, factor_all, tag, coef_slot, slot, name):
+            coef = tile([P, QT], F32, name + "_coef", tag=coef_slot)
             nc.vector.reciprocal(coef[:], den[:])
             turned_w = bank(tag, name + "_turned")
             view = turned_w[:].rearrange("p (u q) -> p u q", u=2)
@@ -171,24 +176,39 @@ def tile_attend_confidencegate_pl_kernel(
             nc.scalar.copy(
                 woven[:].rearrange("p (x j) u -> p x j u", j=QT), view.rearrange("p u (j x) -> p x j u", j=QT)
             )
-            return quantise(woven[:].rearrange("p q u -> p (q u)").bitcast(BF16), name, Q)
+            return woven[:].rearrange("p q u -> p (q u)").bitcast(BF16)
 
-        neg_z, sum_b, probs_b = exps(score_b, "b")
+        neg_z, sum_b, probs_b = exps(score_b, "b", "wkey_raw1")
         odds_against = tile([P, QT], F32, "odds_against")
         odds_for = tile([P, QT], F32, "odds_for")
         for j in range(QT):
             c = slice(j, j + 1)
             nc.scalar.activation(odds_against[:, c], neg_z[:, c], ACT.Exp, bias=steep_th[:, c], scale=steep_c[:, c])
             nc.scalar.activation(odds_for[:, c], neg_z[:, c], ACT.Exp, bias=neg_steep_th[:, c], scale=neg_steep[:, c])
-        neg_max_a, sum_a, probs_a = exps(score_a, "a")
+        den_u = denominators(odds_against, sum_b, "u")
+        neg_max_a, sum_a, probs_a = exps(score_a, "a", "a_probs0")
+        den_w = denominators(odds_for, sum_a, "w")
+        size_all = bank("sb0", "size_all")
+        wf_all = bank("sb1", "wf_all")
+        for k in range(4):
+            nc.tensor.transpose(size_all[:, P * k : P * (k + 1)], size_c[:, k : k + 1].to_broadcast([P, P]), ident[:])
+        for k in range(4):
+            nc.tensor.transpose(wf_all[:, P * k : P * (k + 1)], wf_c[:, k : k + 1].to_broadcast([P, P]), ident[:])
 
-        def values(r, tag, shared, slot):
+        wv_bf = tile([P, PACK, P, PACK], BF16, "wv_bf")
+        for r in range(PACK):
+            nc.gpsimd.tensor_copy(wv_bf[:, r], wval_raw[:].rearrange("p j (s r) -> p r s j", r=PACK)[:, r])
+
+        def values(r, tag, on_scalar, slot):
             picked = tile([P, I], BF16, "picked%d" % r, tag=slot)
-            if shared:
-                nc.scalar.activation(picked[:, 0:256], val_pool[r][:].indirect(offsets[:, 0:16]), ACT.Copy)
-                nc.vector.tensor_copy(picked[:, 256:512], val_pool[r][:].indirect(offsets[:, 16:32]))
-            else:
-                nc.scalar.activation(picked[:], val_pool[r][:].indirect(offsets[:]), ACT.Copy)
+            if on_scalar:
+                nc.scalar.activation(
+                    picked[:, 0:on_scalar], val_pool[r][:].indirect(offsets[:, 0 : on_scalar // 16]), ACT.Copy
+                )
+            if on_scalar < I:
+                nc.vector.tensor_copy(
+                    picked[:, on_scalar:I], val_pool[r][:].indirect(offsets[:, on_scalar // 16 : I // 16])
+                )
             turned_v = bank(tag, "turned_v%d" % r)
             view = turned_v[:, 0:256].rearrange("p (u s) -> p u s", u=2)
             words = picked[:].bitcast(F32)
@@ -198,48 +218,57 @@ def tile_attend_confidencegate_pl_kernel(
             nc.scalar.copy(woven[:], view.rearrange("p u s -> p s u"))
             return woven[:].rearrange("p s u -> p (s u)").bitcast(BF16)
 
-        v_mx = [quantise(values(0, "vt", False, "a_neg_max"), "v0", P)]
-        u_codes, u_scales = weights(probs_b, sum_b, odds_against, size_all, "sb0", reused[0], "u")
-        v_mx.append(quantise(values(1, "sb1", False, "u_bf1"), "v1", P))
-        w_codes, w_scales = weights(probs_a, sum_a, odds_for, wf_all, "vt", reused[1], "w")
-        wv_bf = tile([P, PACK, P, PACK], BF16, "wv_bf", tag="a_probs1")
-        nc.vector.tensor_copy(
-            wv_bf[:].rearrange("p r s j -> p s j r"), wval_raw[:].rearrange("p j (s r) -> p s j r", r=PACK)
-        )
-        wv_codes, wv_scales = quantise(wv_bf[:].rearrange("p r s j -> p (r s j)"), "wval", E)
-        v2_bf = values(2, "size", True, "w_bf1")
+        v0_bf = values(0, "vt", I, "a_neg_max")
+        ut_bf = weights(probs_b, den_u, size_all, "tu", "wk_scales", "val_pool0", "u")
+        wt_bf = weights(probs_a, den_w, wf_all, "tw", "w_coef", "a_neg_max", "w")
+        v1_bf = values(1, "t1", 0, "a_probs1")
+        u_codes, u_scales = quantise(ut_bf, "u", Q, 0)
+        v2_bf = values(2, "sb0", I // 2, "w_bf1")
+        wv_codes, wv_scales = quantise(wv_bf[:].rearrange("p r s j -> p (r s j)"), "wval", E, POOL_BYTES)
+        w_codes, w_scales = quantise(wt_bf, "w", Q, POOL_BYTES + 4 * E)
+        v_mx = [
+            quantise(v0_bf, "v0", P, POOL_BYTES + 4 * (E + Q)),
+            quantise(v1_bf, "v1", P, POOL_BYTES + 4 * (E + Q + P)),
+            quantise(v2_bf, "v2", P),
+        ]
 
         result = [bank("sa%d" % h, "result%d" % h) for h in range(QT)]
 
-        def products(r):
-            es = slice(P * r, P * (r + 1))
+        def window_pass(r, h):
+            es, qs = slice(P * r, P * (r + 1)), slice(P * h, P * (h + 1))
+            nc.tensor.matmul_mx(
+                result[h][:, es], wv_codes[:, es].bitcast(FP8X4), wv_scales[:, es],
+                w_codes[:, qs].bitcast(FP8X4), w_scales[:, qs], start=True, stop=False,
+            )
+
+        def memory_pass(r, h):
+            es, qs = slice(P * r, P * (r + 1)), slice(P * h, P * (h + 1))
             v_codes, v_scales = v_mx[r]
+            nc.tensor.matmul_mx(
+                result[h][:, es], v_codes[:].bitcast(FP8X4), v_scales[:],
+                u_codes[:, qs].bitcast(FP8X4), u_scales[:, qs], start=False, stop=True,
+            )
+
+        def products(r):
             for h in range(QT):
-                qs = slice(P * h, P * (h + 1))
-                nc.tensor.matmul_mx(
-                    result[h][:, es], wv_codes[:, es].bitcast(FP8X4), wv_scales[:, es],
-                    w_codes[:, qs].bitcast(FP8X4), w_scales[:, qs], start=True, stop=False,
-                )
-                nc.tensor.matmul_mx(
-                    result[h][:, es], v_codes[:].bitcast(FP8X4), v_scales[:],
-                    u_codes[:, qs].bitcast(FP8X4), u_scales[:, qs], start=False, stop=True,
-                )
+                window_pass(r, h)
+            for h in range(QT):
+                memory_pass(r, h)
 
         last = PACK - 1
         for r in range(2):
             products(r)
-        v3_bf = values(last, "wf", True, reused[1])
-        v_mx.append(quantise(v2_bf, "v2", P, slot=reused[1]))
-        v_mx.append(quantise(v3_bf, "v3", P))
+        v3_bf = values(last, "sb1", I // 2, "a_neg_max")
         out_dealt = out_0.rearrange("(s r) q -> s r q", r=PACK)
-        o_first = tile([P, 2, Q], F32, "o_first")
+        o_first = placed([P, last, Q], F32, "o_first", 2 * POOL_BYTES)
+        for h, copy in enumerate((nc.vector.tensor_copy, nc.scalar.copy)):
+            copy(o_first[:, 0:2, P * h : P * (h + 1)], result[h][:, 0 : P * 2].rearrange("p (r q) -> p r q", r=2))
+        v_mx.append(quantise(v3_bf, "v3", P))
+        products(2)
         for h in range(QT):
-            nc.vector.tensor_copy(
-                o_first[:, :, P * h : P * (h + 1)], result[h][:, 0 : P * 2].rearrange("p (r q) -> p r q", r=2)
-            )
-        nc.sync.dma_start(out_dealt[:, 0:2, :], o_first[:])
-        for r in range(2, PACK):
-            products(r)
+            nc.scalar.copy(o_first[:, 2, P * h : P * (h + 1)], result[h][:, P * 2 : P * last])
+        nc.sync.dma_start(out_dealt[:, 0:last, :], o_first[:])
+        products(last)
 
         o_codes = tile([P, Q], U32, "o_codes")
         o_scales = tile([P, Q], U8, "o_scales")
@@ -250,12 +279,10 @@ def tile_attend_confidencegate_pl_kernel(
             nc.vector.quantize_mx(
                 out=o_codes[:, qs].bitcast(FP8X4), scales=o_scales[:, qs], in_=o_bf[:].rearrange("p q r -> p (q r)")
             )
-        o_last = tile([P, 2, Q], F32, "o_last")
+        o_last = tile([P, Q], F32, "o_last")
         for h in range(QT):
-            nc.scalar.copy(
-                o_last[:, :, P * h : P * (h + 1)], result[h][:, P * 2 : P * PACK].rearrange("p (r q) -> p r q", r=2)
-            )
-        nc.sync.dma_start(out_dealt[:, 2:PACK, :], o_last[:])
+            nc.scalar.copy(o_last[:, P * h : P * (h + 1)], result[h][:, P * last : P * PACK])
+        nc.sync.dma_start(out_dealt[:, last, :], o_last[:])
 
         nc.sync.dma_start(out_1[0].rearrange("p c t -> p (c t)").bitcast(I32), o_codes[:].bitcast(I32))
         for quad in range(4):

from contextlib import ExitStack

import concourse.mybir as mybir
from concourse.masks import make_identity

D, T, I, Q, E, M = 512, 2048, 512, 256, 512, 512
FLOPS = 2 * 512 * 512 * 256 * 4

F32 = mybir.dt.float32
BF16 = mybir.dt.bfloat16
I32 = mybir.dt.int32
U32 = mybir.dt.uint32
U16 = mybir.dt.uint16
U8 = mybir.dt.uint8
FP8X4 = mybir.dt.float8_e4m3fn_x4
FP4X4 = mybir.dt.float4_e2m1fn_x4
ALU = mybir.AluOpType
ACT = mybir.ActivationFunctionType
AX = mybir.AxisListType

P = 128
PACK = 4
QT = Q // P
POOL_BYTES = 4 * T


def tile_attend_confidencegate_pl_kernel(
    tc, query, wkey, wval, keys_words, keys_scales, vals, th, steep, wf, size, offs, out_0, out_1, out_2
):
    nc = tc.nc
    with ExitStack() as ctx:
        sb = ctx.enter_context(tc.tile_pool(name="sb", bufs=1))
        shared = ctx.enter_context(tc.tile_pool(name="shared", bufs=1))
        ps = ctx.enter_context(tc.psum_pool(name="ps", bufs=1))

        def tile(shape, dtype, name, tag=None):
            return sb.tile(shape, dtype, name=name, tag=tag or name, align_bytes=64)

        def placed(shape, dtype, name, offset):
            return shared.tile(shape, dtype, name=name, tag=name, offset=offset, align_bytes=64)

        def bank(tag, name):
            return ps.tile([P, 512], F32, name=name, tag=tag)

        def quantise(src, name, cols, offset=None):
            if offset is None:
                codes = tile([P, cols], U32, name + "_codes")
            else:
                codes = placed([P, cols], U32, name + "_codes", offset)
            scales = tile([P, cols], U8, name + "_scales")
            nc.vector.quantize_mx(out=codes[:].bitcast(FP8X4), scales=scales[:], in_=src)
            return codes, scales

        key_scale_pool = tile([P, T], U8, "key_scale_pool")
        nc.gpsimd.memset(key_scale_pool[:, 0 : T // 2].bitcast(I32), 0)
        nc.vector.memset(key_scale_pool[:, T // 2 : T].bitcast(I32), 0)
        ident = tile([P, P], F32, "ident")
        make_identity(nc, ident[:])

        offsets = tile([P, I // 16], U16, "offsets")
        nc.sync.dma_start(offsets[:], offs)
        key_pool = tile([P, T], U16, "key_pool")
        nc.sync.dma_start(key_pool[:].bitcast(I32), keys_words[0].bitcast(I32))
        query_raw = tile([P, PACK, Q], F32, "query_raw")
        nc.sync.dma_start(query_raw[:], query.rearrange("(p j) q -> p j q", j=PACK))
        for quad in range(4):
            nc.sync.dma_start(
                key_scale_pool[32 * quad : 32 * quad + 4, :].bitcast(I32),
                keys_scales[0, 4 * quad : 4 * quad + 4, :].bitcast(I32),
            )
        wkey_rows = wkey.rearrange("(p j) m -> p j m", j=PACK)
        wkey_raw = [tile([P, PACK, M // 2], F32, "wkey_raw%d" % half) for half in range(2)]
        for half in range(2):
            nc.sync.dma_start(wkey_raw[half][:], wkey_rows[:, :, half * M // 2 : (half + 1) * M // 2])
        steep_t = tile([P, QT], F32, "steep_t")
        th_t = tile([P, QT], F32, "th_t")
        size_c = tile([P, PACK], F32, "size_c")
        wf_c = tile([P, PACK], F32, "wf_c")
        nc.sync.dma_start(steep_t[:], steep.rearrange("(x j) o -> x (j o)", j=QT))
        nc.sync.dma_start(th_t[:], th.rearrange("(x j) o -> x (j o)", j=QT))
        nc.sync.dma_start(size_c[:], size.rearrange("o (x k) -> (o x) k", k=PACK))
        nc.sync.dma_start(wf_c[:], wf.rearrange("o (x k) -> (o x) k", k=PACK))
        wval_raw = tile([P, PACK, E], F32, "wval_raw")
        nc.sync.dma_start(wval_raw[:], wval.rearrange("(p j) e -> p j e", j=PACK))
        vals_dealt = vals.rearrange("(s r) t -> r s t", r=PACK)
        val_pool = [tile([P, T], F32, "val_pool0")]
        val_pool.extend(placed([P, T], F32, "val_pool%d" % r, POOL_BYTES * (r - 1)) for r in range(1, PACK))
        for r in range(PACK):
            nc.sync.dma_start(val_pool[r][:], vals_dealt[r])
        th_c, steep_c = th_t[:], steep_t[:]

        neg_steep = tile([P, QT], F32, "neg_steep")
        steep_th = tile([P, QT], F32, "steep_th")
        neg_steep_th = tile([P, QT], F32, "neg_steep_th")
        nc.gpsimd.tensor_scalar(neg_steep[:], steep_c, -1.0, 0.0, ALU.mult, ALU.add)
        nc.gpsimd.tensor_tensor(steep_th[:], steep_c, th_c, ALU.mult)
        nc.gpsimd.tensor_tensor(neg_steep_th[:], neg_steep[:], th_c, ALU.mult)

        key_words = tile([P, I], U16, "key_words")
        nc.vector.tensor_copy(key_words[:], key_pool[:].indirect(offsets[:]))
        key_scales = tile([P, I], U8, "key_scales")
        nc.vector.tensor_copy(key_scales[:], key_scale_pool[:].indirect(offsets[:]))
        query_bf = tile([P, Q, PACK], BF16, "query_bf")
        nc.scalar.activation(
            query_bf[:].rearrange("p (j x) t -> p x t j", j=QT),
            query_raw[:].rearrange("p t (x j) -> p x t j", j=QT),
            ACT.Copy,
        )
        q_codes, q_scales = quantise(query_bf[:].rearrange("p c t -> p (c t)"), "query", Q)

        score_b = [bank("sb%d" % j, "score_b%d" % j) for j in range(QT)]
        for j in range(QT):
            qs = slice(P * j, P * (j + 1))
            nc.tensor.matmul_mx(
                score_b[j][:], q_codes[:, qs].bitcast(FP8X4), q_scales[:, qs],
                key_words[:].bitcast(FP4X4), key_scales[:], start=True, stop=True,
            )

        wk_codes = tile([P, M], U32, "wk_codes")
        wk_scales = tile([P, M], U8, "wk_scales")
        for half in range(2):
            ms = slice(half * M // 2, (half + 1) * M // 2)
            wk_bf = tile([P, M // 2, PACK], BF16, "wk_bf%d" % half)
            nc.scalar.copy(
                wk_bf[:].rearrange("p (c i) t -> p c t i", i=4),
                wkey_raw[half][:].rearrange("p t (c i) -> p c t i", i=4),
            )
            nc.vector.quantize_mx(
                out=wk_codes[:, ms].bitcast(FP8X4), scales=wk_scales[:, ms], in_=wk_bf[:].rearrange("p c t -> p (c t)")
            )
        score_a = [bank("sa%d" % j, "score_a%d" % j) for j in range(QT)]
        for j in range(QT):
            qs = slice(P * j, P * (j + 1))
            nc.tensor.matmul_mx(
                score_a[j][:], q_codes[:, qs].bitcast(FP8X4), q_scales[:, qs],
                wk_codes[:].bitcast(FP8X4), wk_scales[:], start=True, stop=True,
            )

        def exps(score, name, slot):
            neg_max = tile([P, QT], F32, name + "_neg_max")
            sums = tile([P, QT], F32, name + "_sums")
            probs = [tile([P, 512], F32, name + "_probs0", tag=slot), tile([P, 512], F32, name + "_probs1")]
            for j in range(QT):
                nc.vector.tensor_reduce(neg_max[:, j : j + 1], score[j][:], AX.X, ALU.max, negate=True)
                nc.scalar.activation(
                    probs[j][:], score[j][:], ACT.Exp, bias=neg_max[:, j : j + 1], accum_out=sums[:, j : j + 1]
                )
            return neg_max, sums, probs

        def denominators(odds, sums, name):
            den = tile([P, QT], F32, name + "_den")
            for j in range(QT):
                c = slice(j, j + 1)
                nc.scalar.activation(den[:, c], odds[:, c], ACT.Identity, bias=sums[:, c], scale=sums[:, c])
            return den

        def weights(probs, den, factor_all, tag, coef_slot, slot, name):
            coef = tile([P, QT], F32, name + "_coef", tag=coef_slot)
            nc.vector.reciprocal(coef[:], den[:])
            turned_w = bank(tag, name + "_turned")
            view = turned_w[:].rearrange("p (u q) -> p u q", u=2)
            for j in range(QT):
                w_bf = tile([P, 512], BF16, name + "_bf%d" % j)
                nc.vector.scalar_tensor_tensor(
                    w_bf[:].rearrange("p (x k) -> p x k", k=PACK),
                    probs[j][:].rearrange("p (x k) -> p x k", k=PACK),
                    coef[:, j : j + 1],
                    factor_all[:].rearrange("p (k x) -> p x k", k=PACK),
                    ALU.mult,
                    ALU.mult,
                )
                words = w_bf[:].bitcast(F32)
                for u in range(2):
                    nc.tensor.transpose(view[:, u, P * j : P * (j + 1)], words[:, u::2], ident[:])
            woven = tile([P, Q, 2], F32, name + "_woven", tag=slot)
            nc.scalar.copy(
                woven[:].rearrange("p (x j) u -> p x j u", j=QT), view.rearrange("p u (j x) -> p x j u", j=QT)
            )
            return woven[:].rearrange("p q u -> p (q u)").bitcast(BF16)

        neg_z, sum_b, probs_b = exps(score_b, "b", "wkey_raw1")
        odds_against = tile([P, QT], F32, "odds_against")
        odds_for = tile([P, QT], F32, "odds_for")
        for j in range(QT):
            c = slice(j, j + 1)
            nc.scalar.activation(odds_against[:, c], neg_z[:, c], ACT.Exp, bias=steep_th[:, c], scale=steep_c[:, c])
            nc.scalar.activation(odds_for[:, c], neg_z[:, c], ACT.Exp, bias=neg_steep_th[:, c], scale=neg_steep[:, c])
        den_u = denominators(odds_against, sum_b, "u")
        neg_max_a, sum_a, probs_a = exps(score_a, "a", "a_probs0")
        den_w = denominators(odds_for, sum_a, "w")
        size_all = bank("sb0", "size_all")
        wf_all = bank("sb1", "wf_all")
        for k in range(4):
            nc.tensor.transpose(size_all[:, P * k : P * (k + 1)], size_c[:, k : k + 1].to_broadcast([P, P]), ident[:])
        for k in range(4):
            nc.tensor.transpose(wf_all[:, P * k : P * (k + 1)], wf_c[:, k : k + 1].to_broadcast([P, P]), ident[:])

        wv_bf = tile([P, PACK, P, PACK], BF16, "wv_bf")
        for r in range(PACK):
            nc.gpsimd.tensor_copy(wv_bf[:, r], wval_raw[:].rearrange("p j (s r) -> p r s j", r=PACK)[:, r])

        def values(r, tag, on_scalar, slot):
            picked = tile([P, I], BF16, "picked%d" % r, tag=slot)
            if on_scalar:
                nc.scalar.activation(
                    picked[:, 0:on_scalar], val_pool[r][:].indirect(offsets[:, 0 : on_scalar // 16]), ACT.Copy
                )
            if on_scalar < I:
                nc.vector.tensor_copy(
                    picked[:, on_scalar:I], val_pool[r][:].indirect(offsets[:, on_scalar // 16 : I // 16])
                )
            turned_v = bank(tag, "turned_v%d" % r)
            view = turned_v[:, 0:256].rearrange("p (u s) -> p u s", u=2)
            words = picked[:].bitcast(F32)
            for u in range(2):
                nc.tensor.transpose(view[:, u, :], words[:, u::2], ident[:])
            woven = tile([P, P, 2], F32, "v_woven%d" % r)
            nc.scalar.copy(woven[:], view.rearrange("p u s -> p s u"))
            return woven[:].rearrange("p s u -> p (s u)").bitcast(BF16)

        v0_bf = values(0, "vt", I, "a_neg_max")
        ut_bf = weights(probs_b, den_u, size_all, "tu", "wk_scales", "val_pool0", "u")
        wt_bf = weights(probs_a, den_w, wf_all, "tw", "w_coef", "a_neg_max", "w")
        v1_bf = values(1, "t1", 0, "a_probs1")
        u_codes, u_scales = quantise(ut_bf, "u", Q, 0)
        v2_bf = values(2, "sb0", I // 2, "w_bf1")
        wv_codes, wv_scales = quantise(wv_bf[:].rearrange("p r s j -> p (r s j)"), "wval", E, POOL_BYTES)
        w_codes, w_scales = quantise(wt_bf, "w", Q, POOL_BYTES + 4 * E)
        v_mx = [
            quantise(v0_bf, "v0", P, POOL_BYTES + 4 * (E + Q)),
            quantise(v1_bf, "v1", P, POOL_BYTES + 4 * (E + Q + P)),
            quantise(v2_bf, "v2", P),
        ]

        result = [bank("sa%d" % h, "result%d" % h) for h in range(QT)]

        def window_pass(r, h):
            es, qs = slice(P * r, P * (r + 1)), slice(P * h, P * (h + 1))
            nc.tensor.matmul_mx(
                result[h][:, es], wv_codes[:, es].bitcast(FP8X4), wv_scales[:, es],
                w_codes[:, qs].bitcast(FP8X4), w_scales[:, qs], start=True, stop=False,
            )

        def memory_pass(r, h):
            es, qs = slice(P * r, P * (r + 1)), slice(P * h, P * (h + 1))
            v_codes, v_scales = v_mx[r]
            nc.tensor.matmul_mx(
                result[h][:, es], v_codes[:].bitcast(FP8X4), v_scales[:],
                u_codes[:, qs].bitcast(FP8X4), u_scales[:, qs], start=False, stop=True,
            )

        def products(r):
            for h in range(QT):
                window_pass(r, h)
            for h in range(QT):
                memory_pass(r, h)

        last = PACK - 1
        for r in range(2):
            products(r)
        v3_bf = values(last, "sb1", I // 2, "a_neg_max")
        out_dealt = out_0.rearrange("(s r) q -> s r q", r=PACK)
        o_first = placed([P, last, Q], F32, "o_first", 2 * POOL_BYTES)
        for h, copy in enumerate((nc.vector.tensor_copy, nc.scalar.copy)):
            copy(o_first[:, 0:2, P * h : P * (h + 1)], result[h][:, 0 : P * 2].rearrange("p (r q) -> p r q", r=2))
        v_mx.append(quantise(v3_bf, "v3", P))
        products(2)
        for h in range(QT):
            nc.scalar.copy(o_first[:, 2, P * h : P * (h + 1)], result[h][:, P * 2 : P * last])
        nc.sync.dma_start(out_dealt[:, 0:last, :], o_first[:])
        products(last)

        o_codes = tile([P, Q], U32, "o_codes")
        o_scales = tile([P, Q], U8, "o_scales")
        for h, copy in enumerate((nc.vector.tensor_copy, nc.scalar.copy)):
            qs = slice(P * h, P * (h + 1))
            o_bf = tile([P, P, PACK], BF16, "o_bf%d" % h)
            copy(o_bf[:], result[h][:].rearrange("p (r q) -> p q r", r=PACK))
            nc.vector.quantize_mx(
                out=o_codes[:, qs].bitcast(FP8X4), scales=o_scales[:, qs], in_=o_bf[:].rearrange("p q r -> p (q r)")
            )
        o_last = tile([P, Q], F32, "o_last")
        for h in range(QT):
            nc.scalar.copy(o_last[:, P * h : P * (h + 1)], result[h][:, P * last : P * PACK])
        nc.sync.dma_start(out_dealt[:, last, :], o_last[:])

        nc.sync.dma_start(out_1[0].rearrange("p c t -> p (c t)").bitcast(I32), o_codes[:].bitcast(I32))
        for quad in range(4):
            queue = nc.scalar if quad % 2 else nc.sync
            queue.dma_start(
                out_2[0, 4 * quad : 4 * quad + 4, :].bitcast(I32), o_scales[32 * quad : 32 * quad + 4, :].bitcast(I32)
            )
